import numpy as np, ml_dtypes
CORES = [24,40,56,80,88,96]
N = 6
import mx_ref
KO = 2
F = np.float32(1.3)
OWN = [0,0,0,0,0,0]
BF = ml_dtypes.bfloat16
def tile(rs):
    return np.stack(rs, axis=2).reshape(128, -1).astype(BF)
def pick(b):
    s = np.zeros((128, 128, 4), np.float32)
    s[np.arange(128), np.arange(128), b] = 1.0
    return mx_ref.quantize(s.reshape(128, 512).astype(BF))
def pk(c, s, i=0):
    return (np.ascontiguousarray(c[:, 512 * i:512 * i + 512]), mx_ref.live(s[:, 128 * i:128 * i + 128]))
def inputs(rng, e, E):
    def f(*shape):
        v = (rng.standard_normal(shape, dtype=np.float32) * np.exp2(rng.integers(-2, 3, shape[:-1] + (1,)))).astype(BF)
        return mx_ref.spread((v.astype(np.float32) * np.exp2(rng.integers(-E, E + 1, shape[:-2] + (1, 1))).astype(np.float32)).astype(BF), rng, e)
    def packed(k):
        c = np.zeros((N, 128, k * 512), np.uint8); s = np.zeros((N, 128, k * 128), np.uint8)
        for r in range(N):
            for i in range(k):
                a, b = mx_ref.quantize(f(128, 512)); c[r][:, 512 * i:512 * i + 512] = a; s[r][:, 128 * i:128 * i + 128] = mx_ref.plane(b, rng)
        return c, s
    d = {}
    d["kc"], d["ks"] = packed(KO)
    d["q"] = f(N, 128, 512)
    return d
def setup_inputs(rng):
    return inputs(rng, 0, 0)
def setup_inputs_blocks(rng):
    return inputs(rng, 4, 0)
def setup_inputs_wide(rng):
    return inputs(rng, 0, 8)
def reference(kc, ks, q):
    S = [pick(t) for t in range(4)]
    anew = lambda p, i: mx_ref.quantize(tile([mx_ref.matmul(S[t], pk(kc[p], ks[p], i)) * F for t in range(4)]))
    y = np.full((N, 128, 1536), np.nan, np.float32)
    for o in range(N):
        if OWN[o] != o: continue
        qq = mx_ref.quantize(q[o])
        M = [pk(kc[o], ks[o], i) for i in range(KO)] + [anew(p, i) for p in range(N) if p != o and OWN[p] == o for i in range(KO)]
        y[o][:, :128 * len(M)] = np.concatenate([mx_ref.matmul(qq, m) for m in M], axis=1)
    return {"y": y}

@@ -1,0 +1,184 @@
+import numpy as np
+from concourse.mybir import dt, AluOpType, ActivationFunctionType
+
+NT = 2
+W = 128
+SIM = 112
+F = float(np.float32(1.3))
+
+SCRATCH = {
+    "kin": ("sbuf", [128, NT * W], "float8_e4m3fn_x4"),
+    "kins": ("sbuf", [128, NT * W], "uint8"),
+    "e": ("sbuf", [128, 4 * W + 4], "bfloat16"),
+    "sc": ("sbuf", [128, 4 * W], "float8_e4m3fn_x4"),
+    "ss": ("sbuf", [128, 4 * W], "uint8"),
+    "h": ("sbuf", [128, 4 * NT * W], "bfloat16"),
+    "kq": ("sbuf", [128, NT * W], "float8_e4m3fn_x4"),
+    "kqs": ("sbuf", [128, NT * W], "uint8"),
+    "rc": ("sbuf", [128, W], "float8_e4m3fn_x4"),
+    "rs": ("sbuf", [128, NT * W], "uint8"),
+    "qb": ("sbuf", [128, 4 * W], "bfloat16"),
+    "qc": ("sbuf", [128, W], "float8_e4m3fn_x4"),
+    "qs": ("sbuf", [128, W], "uint8"),
+    "lc": ("sbuf", [128, 6 * NT * W], "float8_e4m3fn_x4"),
+    "ls": ("sbuf", [128, 6 * NT * W], "uint8"),
+    "yb": ("sbuf", [128, 6 * NT * W], "float32"),
+    "ps": ("psum", [128, 8 * 512], "float32"),
+}
+SEMAPHORES = (["zero", "diag", "sel", "kp", "mm", "hv", "ha", "quant", "sent", "rca", "rsa", "qin", "qq", "cv", "ca",
+               "outv", "outa"] + ["kc%d" % i for i in range(NT)] + ["arr%d" % r for r in range(6)])
+
+
+def engines(mask, n):
+    out, bit = 0, 1
+    while n:
+        if mask & bit:
+            out |= bit
+            n -= 1
+        bit <<= 1
+    return out
+
+
+def count(mask):
+    return bin(mask).count("1")
+
+
+def relays_of(topo, p, o):
+    if topo.may_write(p, o):
+        return []
+    c = [x for x in range(SIM) if x != p and topo.chip(x) == topo.chip(p) and topo.may_write(x, o)]
+    c.sort(key=lambda x: (topo.die(x) == topo.die(p), x))
+    return c[:2]
+
+
+def rank_program(g, core, T, topo):
+    cores, own = T.cores, T.tables["OWN"]
+    rank = T.rank_of(core)
+    NE = 8
+
+    def send(out, in_, rsem, dst):
+        rid, pid, _ = topo.addr(dst)
+        m = engines(topo.mask(core, dst), NE)
+        g.remote_dma(out, in_, T.sem[rsem], T.sem.sent, pid, rid, m)
+        return count(m)
+
+    def codes(buf, a, n):
+        return buf[:, a:a + n].bitcast(dt.uint8)
+
+    if rank is None:
+        for r in range(len(cores)):
+            o = cores[own[r]]
+            if own[r] == r:
+                continue
+            rel = relays_of(topo, cores[r], o)
+            if core in rel:
+                i, at = rel.index(core), r * NT * W
+                g.wait_ge(T.sem.rca, NE)
+                n = send(codes(T.lc, at + i * W, W), codes(T.rc, 0, W), "arr%d" % r, o)
+                if i == 0:
+                    g.wait_ge(T.sem.rsa, NE)
+                    n += send(T.ls[:, at:at + NT * W], T.rs[:, :], "arr%d" % r, o)
+                g.wait_ge(T.sem.sent, n)
+        return
+
+    if own[rank] != rank:
+        producer(g, T, topo, cores[own[rank]], rank, core, send, codes)
+    else:
+        prods = [r for r in range(len(cores)) if r != rank and own[r] == rank]
+        consumer(g, T, topo, rank, core, prods, NE)
+
+
+def load_k(g, T):
+    kin, kc = T.kin, T.kc
+    for i in range(NT):
+        g.sync.dma_start(kin[:, i * W:(i + 1) * W].bitcast(dt.uint8),
+                         kc[:, 4 * i * W:4 * (i + 1) * W]).then_inc(T.sem["kc%d" % i], 16)
+    g.scalar.dma_start(T.kins[:, :], T.ks[:, :]).then_inc(T.sem.kp, 16)
+
+
+def producer(g, T, topo, o, rank, core, send, codes):
+    load_k(g, T)
+    g.vector.memset(T.e[:, :], 0.0).then_inc(T.sem.zero, 1)
+    g.wait_ge(T.sem.zero, 1)
+    d = T.e[:, 3:4 * W + 3:4]
+    g.affine_select(d, d, [[-1, W]], AluOpType.not_equal, 1.0, 0, 1).then_inc(T.sem.diag, 1)
+    g.vector.wait_ge(T.sem.diag, 1)
+    for b in range(4):
+        g.vector.quantize_mx(T.sc[:, b * W:(b + 1) * W], T.ss[:, b * W:(b + 1) * W],
+                             T.e[:, 3 - b:3 - b + 4 * W]).then_inc(T.sem.sel, 1)
+    g.tensor.wait_ge(T.sem.kp, 16)
+    for i in range(NT):
+        g.tensor.wait_ge(T.sem["kc%d" % i], 16)
+        for b in range(4):
+            if i == 0:
+                g.tensor.wait_ge(T.sem.sel, b + 1)
+            at = (4 * i + b) * 512
+            g.tensor.matmul_mx(T.ps[:, at:at + W], T.sc[:, b * W:(b + 1) * W], T.ss[:, b * W:(b + 1) * W],
+                               T.kin[:, i * W:(i + 1) * W], T.kins[:, i * W:(i + 1) * W], True, True).then_inc(T.sem.mm, 1)
+    for i in range(NT):
+        for b in range(4):
+            at, to = (4 * i + b) * 512, 4 * i * W
+            out, in_ = T.h[:, to + b:to + 4 * W:4], T.ps[:, at:at + W]
+            if b % 2 == 0:
+                g.vector.wait_ge(T.sem.mm, 4 * i + b + 1)
+                g.vector.tensor_scalar(out, in_, F, None, AluOpType.mult).then_inc(T.sem.hv, 1)
+            else:
+                g.scalar.wait_ge(T.sem.mm, 4 * i + b + 1)
+                g.scalar.activation(out, in_, ActivationFunctionType.Copy, scale=F).then_inc(T.sem.ha, 1)
+        g.vector.wait_ge(T.sem.hv, 2 * (i + 1))
+        g.vector.wait_ge(T.sem.ha, 2 * (i + 1))
+        g.vector.quantize_mx(T.kq[:, i * W:(i + 1) * W], T.kqs[:, i * W:(i + 1) * W],
+                             T.h[:, 4 * i * W:4 * (i + 1) * W]).then_inc(T.sem.quant, 1)
+    rel, at, n = relays_of(topo, core, o), rank * NT * W, 0
+    for i in range(NT):
+        g.wait_ge(T.sem.quant, i + 1)
+        if rel:
+            n += send(codes(T.rc, 0, W), codes(T.kq, i * W, W), "rca", rel[i])
+        else:
+            n += send(codes(T.lc, at + i * W, W), codes(T.kq, i * W, W), "arr%d" % rank, o)
+    if rel:
+        n += send(T.rs[:, :], T.kqs[:, :], "rsa", rel[0])
+    else:
+        n += send(T.ls[:, at:at + NT * W], T.kqs[:, :], "arr%d" % rank, o)
+    g.wait_ge(T.sem.sent, n)
+
+
+def consumer(g, T, topo, rank, core, prods, ne):
+    g.scalar.dma_start(T.qb[:, :], T.q[:, :]).then_inc(T.sem.qin, 16)
+    load_k(g, T)
+    g.vector.wait_ge(T.sem.qin, 16)
+    g.vector.quantize_mx(T.qc[:, :], T.qs[:, :], T.qb[:, :]).then_inc(T.sem.qq, 1)
+    order = [rank] + sorted(prods, key=lambda r: (len(relays_of(topo, T.cores[r], core)), r))
+    place = [rank] + prods
+    g.tensor.wait_ge(T.sem.qq, 1)
+    g.tensor.wait_ge(T.sem.kp, 16)
+    t = 0
+    for k, r in enumerate(order):
+        if k > 0:
+            g.tensor.wait_ge(T.sem["arr%d" % r], (NT + 1) * ne)
+        for i in range(NT):
+            if k == 0:
+                g.tensor.wait_ge(T.sem["kc%d" % i], 16)
+                c, s = T.kin[:, i * W:(i + 1) * W], T.kins[:, i * W:(i + 1) * W]
+            else:
+                at = (r * NT + i) * W
+                c, s = T.lc[:, at:at + W], T.ls[:, at:at + W]
+            bank = (t % 8) * 512
+            ps, col = T.ps[:, bank:bank + W], (place.index(r) * NT + i) * W
+            if t >= 8:
+                g.tensor.wait_ge(T.sem.cv if i == 0 else T.sem.ca, (t - 8) // 2 + 1)
+            g.tensor.matmul_mx(ps, T.qc[:, :], T.qs[:, :], c, s, True, True).then_inc(T.sem.mm, 1)
+            yb, y = T.yb[:, col:col + W], T.y[:, col:col + W]
+            if i == 0:
+                g.vector.wait_ge(T.sem.mm, t + 1)
+                g.vector.tensor_copy(yb, ps).then_inc(T.sem.cv, 1)
+                g.sync.wait_ge(T.sem.cv, k + 1)
+                g.sync.dma_start(y, yb).then_inc(T.sem.outv, 16)
+            else:
+                g.scalar.wait_ge(T.sem.mm, t + 1)
+                g.scalar.activation(yb, ps, ActivationFunctionType.Copy).then_inc(T.sem.ca, 1)
+                g.scalar.wait_ge(T.sem.ca, k + 1)
+                g.scalar.dma_start(y, yb).then_inc(T.sem.outa, 16)
+            t += 1
+    g.sync.wait_ge(T.sem.outv, 16 * len(order))
+    g.scalar.wait_ge(T.sem.outa, 16 * len(order))

@@ -5,17 +5,20 @@ NT = 2
 W = 128
 SIM = 112
 F = float(np.float32(1.3))
+HALF = W // 2
+PIECES = ["c0", "p", "c1"]
 
 SCRATCH = {
     "kin": ("sbuf", [128, NT * W], "float8_e4m3fn_x4"),
     "kins": ("sbuf", [128, NT * W], "uint8"),
+    "w": ("sbuf", [128, HALF], "bfloat16"),
     "e": ("sbuf", [128, 4 * W + 4], "bfloat16"),
     "sc": ("sbuf", [128, 4 * W], "float8_e4m3fn_x4"),
     "ss": ("sbuf", [128, 4 * W], "uint8"),
     "h": ("sbuf", [128, 4 * NT * W], "bfloat16"),
     "kq": ("sbuf", [128, NT * W], "float8_e4m3fn_x4"),
     "kqs": ("sbuf", [128, NT * W], "uint8"),
-    "rc": ("sbuf", [128, W], "float8_e4m3fn_x4"),
+    "rc": ("sbuf", [128, NT * W], "float8_e4m3fn_x4"),
     "rs": ("sbuf", [128, NT * W], "uint8"),
     "qb": ("sbuf", [128, 4 * W], "bfloat16"),
     "qc": ("sbuf", [128, W], "float8_e4m3fn_x4"),
@@ -25,67 +28,96 @@ SCRATCH = {
     "yb": ("sbuf", [128, 6 * NT * W], "float32"),
     "ps": ("psum", [128, 8 * 512], "float32"),
 }
-SEMAPHORES = (["zero", "diag", "sel", "kp", "mm", "hv", "ha", "quant", "sent", "rca", "rsa", "qin", "qq", "cv", "ca",
-               "outv", "outa"] + ["kc%d" % i for i in range(NT)] + ["arr%d" % r for r in range(6)])
+SEMAPHORES = (["zero", "cnt", "diag", "sel", "kp", "mm", "hv", "ha", "quant", "sent", "qin", "qq", "cv", "ca", "out"]
+              + ["kc%d" % i for i in range(NT)] + ["relay_" + x for x in PIECES]
+              + ["arr%d_%s" % (r, x) for r in range(6) for x in PIECES])
 
 
-def engines(mask, n):
-    out, bit = 0, 1
-    while n:
-        if mask & bit:
-            out |= bit
-            n -= 1
-        bit <<= 1
-    return out
+def engines(topo, src, dst, piece):
+    m = topo.mask(src, dst)
+    for x in range(SIM):
+        if topo.chip(x) != topo.chip(src) and topo.may_write(src, x):
+            m &= topo.mask(src, x)
+            break
+    bits = [b for b in range(16) if m >> b & 1]
+    return sum(1 << b for b in bits[(1 if piece == "c1" else 0)::2])
 
 
 def count(mask):
     return bin(mask).count("1")
 
 
-def relays_of(topo, p, o):
-    if topo.may_write(p, o):
-        return []
-    c = [x for x in range(SIM) if x != p and topo.chip(x) == topo.chip(p) and topo.may_write(x, o)]
-    c.sort(key=lambda x: (topo.die(x) == topo.die(p), x))
-    return c[:2]
+def roads_of(topo, cores, o, prods):
+    far, near, road = 0, 0, {}
+    gates = [x for x in range(SIM) if topo.mates(topo.chip(x), topo.chip(o)) and topo.may_write(x, o)]
+    for r in prods:
+        p = cores[r]
+        other = [x for x in range(SIM) if topo.chip(x) == topo.chip(p) and topo.die(x) != topo.die(p)
+                 and topo.may_write(x, o)]
+        for x in PIECES:
+            road[r, x] = None
+        if topo.may_write(p, o):
+            if near == 0:
+                road[r, "c0"] = other[0]
+            near += 1
+        else:
+            same = far % 2 == 1
+            gate = [x for x in gates if (topo.die(x) == topo.die(o)) == same][0]
+            for x in PIECES:
+                road[r, x] = other[0] if x == "c0" and not same else gate
+            far += 1
+    return road
 
 
 def rank_program(g, core, T, topo):
     cores, own = T.cores, T.tables["OWN"]
     rank = T.rank_of(core)
-    NE = 8
 
-    def send(out, in_, rsem, dst):
+    def send(out, in_, rsem, dst, piece):
         rid, pid, _ = topo.addr(dst)
-        m = engines(topo.mask(core, dst), NE)
+        m = engines(topo, core, dst, piece)
         g.remote_dma(out, in_, T.sem[rsem], T.sem.sent, pid, rid, m)
         return count(m)
 
-    def codes(buf, a, n):
-        return buf[:, a:a + n].bitcast(dt.uint8)
+    def view(codes, planes, at, piece):
+        if piece == "p":
+            return planes[:, at:at + NT * W]
+        a = at + int(piece[1:]) * W
+        return codes[:, a:a + W].bitcast(dt.uint8)
+
+    def prods_of(o):
+        return [r for r in range(len(cores)) if r != o and own[r] == o]
 
     if rank is None:
-        for r in range(len(cores)):
-            o = cores[own[r]]
-            if own[r] == r:
+        n = 0
+        for o in range(len(cores)):
+            if own[o] != o:
                 continue
-            rel = relays_of(topo, cores[r], o)
-            if core in rel:
-                i, at = rel.index(core), r * NT * W
-                g.wait_ge(T.sem.rca, NE)
-                n = send(codes(T.lc, at + i * W, W), codes(T.rc, 0, W), "arr%d" % r, o)
-                if i == 0:
-                    g.wait_ge(T.sem.rsa, NE)
-                    n += send(T.ls[:, at:at + NT * W], T.rs[:, :], "arr%d" % r, o)
-                g.wait_ge(T.sem.sent, n)
+            road = roads_of(topo, cores, cores[o], prods_of(o))
+            for x in PIECES:
+                for r in prods_of(o):
+                    if road[r, x] == core:
+                        g.wait_ge(T.sem["relay_" + x], count(engines(topo, cores[r], core, x)))
+                        n += send(view(T.lc, T.ls, r * NT * W, x), view(T.rc, T.rs, 0, x), "arr%d_%s" % (r, x),
+                                  cores[o], x)
+        if n:
+            g.wait_ge(T.sem.sent, n)
         return
 
-    if own[rank] != rank:
-        producer(g, T, topo, cores[own[rank]], rank, core, send, codes)
-    else:
-        prods = [r for r in range(len(cores)) if r != rank and own[r] == rank]
-        consumer(g, T, topo, rank, core, prods, NE)
+    if own[rank] == rank:
+        consumer(g, T, topo, rank, core, prods_of(rank))
+        return
+    make(g, T)
+    o = cores[own[rank]]
+    road, n = roads_of(topo, cores, o, prods_of(own[rank])), 0
+    for x in PIECES:
+        g.wait_ge(T.sem.quant, 1 if x == "c0" else NT)
+        via, src = road[rank, x], view(T.kq, T.kqs, 0, x)
+        if via is None:
+            n += send(view(T.lc, T.ls, rank * NT * W, x), src, "arr%d_%s" % (rank, x), o, x)
+        else:
+            n += send(view(T.rc, T.rs, 0, x), src, "relay_" + x, via, x)
+    g.wait_ge(T.sem.sent, n)
 
 
 def load_k(g, T):
@@ -96,13 +128,17 @@ def load_k(g, T):
     g.scalar.dma_start(T.kins[:, :], T.ks[:, :]).then_inc(T.sem.kp, 16)
 
 
-def producer(g, T, topo, o, rank, core, send, codes):
+def make(g, T):
     load_k(g, T)
+    g.iota(T.w[:, :], [[-1, HALF]], 0, 1, allow_small_or_imprecise_dtypes=True).then_inc(T.sem.cnt, 1)
     g.vector.memset(T.e[:, :], 0.0).then_inc(T.sem.zero, 1)
-    g.wait_ge(T.sem.zero, 1)
-    d = T.e[:, 3:4 * W + 3:4]
-    g.affine_select(d, d, [[-1, W]], AluOpType.not_equal, 1.0, 0, 1).then_inc(T.sem.diag, 1)
-    g.vector.wait_ge(T.sem.diag, 1)
+    g.vector.wait_ge(T.sem.zero, 1)
+    g.vector.wait_ge(T.sem.cnt, 1)
+    for a in range(2):
+        at = 3 + 4 * HALF * a
+        g.vector.tensor_scalar(T.e[:, at:at + 4 * HALF:4], T.w[:, :], float(HALF * a), None,
+                               AluOpType.is_equal).then_inc(T.sem.diag, 1)
+    g.vector.wait_ge(T.sem.diag, 2)
     for b in range(4):
         g.vector.quantize_mx(T.sc[:, b * W:(b + 1) * W], T.ss[:, b * W:(b + 1) * W],
                              T.e[:, 3 - b:3 - b + 4 * W]).then_inc(T.sem.sel, 1)
@@ -129,56 +165,42 @@ def producer(g, T, topo, o, rank, core, send, codes):
         g.vector.wait_ge(T.sem.ha, 2 * (i + 1))
         g.vector.quantize_mx(T.kq[:, i * W:(i + 1) * W], T.kqs[:, i * W:(i + 1) * W],
                              T.h[:, 4 * i * W:4 * (i + 1) * W]).then_inc(T.sem.quant, 1)
-    rel, at, n = relays_of(topo, core, o), rank * NT * W, 0
-    for i in range(NT):
-        g.wait_ge(T.sem.quant, i + 1)
-        if rel:
-            n += send(codes(T.rc, 0, W), codes(T.kq, i * W, W), "rca", rel[i])
-        else:
-            n += send(codes(T.lc, at + i * W, W), codes(T.kq, i * W, W), "arr%d" % rank, o)
-    if rel:
-        n += send(T.rs[:, :], T.kqs[:, :], "rsa", rel[0])
-    else:
-        n += send(T.ls[:, at:at + NT * W], T.kqs[:, :], "arr%d" % rank, o)
-    g.wait_ge(T.sem.sent, n)
 
 
-def consumer(g, T, topo, rank, core, prods, ne):
+def consumer(g, T, topo, rank, core, prods):
     g.scalar.dma_start(T.qb[:, :], T.q[:, :]).then_inc(T.sem.qin, 16)
     load_k(g, T)
     g.vector.wait_ge(T.sem.qin, 16)
     g.vector.quantize_mx(T.qc[:, :], T.qs[:, :], T.qb[:, :]).then_inc(T.sem.qq, 1)
-    order = [rank] + sorted(prods, key=lambda r: (len(relays_of(topo, T.cores[r], core)), r))
+    road = roads_of(topo, T.cores, core, prods)
+    tiles = [(r, i) for i in range(NT) for r in prods]
+    order = ([(rank, i) for i in range(NT)] + [t for t in tiles if road[t[0], "c%d" % t[1]] is None]
+             + [t for t in tiles if road[t[0], "c%d" % t[1]] is not None])
     place = [rank] + prods
     g.tensor.wait_ge(T.sem.qq, 1)
     g.tensor.wait_ge(T.sem.kp, 16)
-    t = 0
-    for k, r in enumerate(order):
-        if k > 0:
-            g.tensor.wait_ge(T.sem["arr%d" % r], (NT + 1) * ne)
-        for i in range(NT):
-            if k == 0:
-                g.tensor.wait_ge(T.sem["kc%d" % i], 16)
-                c, s = T.kin[:, i * W:(i + 1) * W], T.kins[:, i * W:(i + 1) * W]
-            else:
-                at = (r * NT + i) * W
-                c, s = T.lc[:, at:at + W], T.ls[:, at:at + W]
-            bank = (t % 8) * 512
-            ps, col = T.ps[:, bank:bank + W], (place.index(r) * NT + i) * W
-            if t >= 8:
-                g.tensor.wait_ge(T.sem.cv if i == 0 else T.sem.ca, (t - 8) // 2 + 1)
-            g.tensor.matmul_mx(ps, T.qc[:, :], T.qs[:, :], c, s, True, True).then_inc(T.sem.mm, 1)
-            yb, y = T.yb[:, col:col + W], T.y[:, col:col + W]
-            if i == 0:
-                g.vector.wait_ge(T.sem.mm, t + 1)
-                g.vector.tensor_copy(yb, ps).then_inc(T.sem.cv, 1)
-                g.sync.wait_ge(T.sem.cv, k + 1)
-                g.sync.dma_start(y, yb).then_inc(T.sem.outv, 16)
-            else:
-                g.scalar.wait_ge(T.sem.mm, t + 1)
-                g.scalar.activation(yb, ps, ActivationFunctionType.Copy).then_inc(T.sem.ca, 1)
-                g.scalar.wait_ge(T.sem.ca, k + 1)
-                g.scalar.dma_start(y, yb).then_inc(T.sem.outa, 16)
-            t += 1
-    g.sync.wait_ge(T.sem.outv, 16 * len(order))
-    g.scalar.wait_ge(T.sem.outa, 16 * len(order))
+    for k, (r, i) in enumerate(order):
+        if r == rank:
+            g.tensor.wait_ge(T.sem["kc%d" % i], 16)
+            c, s = T.kin[:, i * W:(i + 1) * W], T.kins[:, i * W:(i + 1) * W]
+        else:
+            for x in ("p", "c%d" % i):
+                src = T.cores[r] if road[r, x] is None else road[r, x]
+                g.tensor.wait_ge(T.sem["arr%d_%s" % (r, x)], count(engines(topo, src, core, x)))
+            at = (r * NT + i) * W
+            c, s = T.lc[:, at:at + W], T.ls[:, at:at + W]
+        bank, col = (k % 8) * 512, (place.index(r) * NT + i) * W
+        ps, yb = T.ps[:, bank:bank + W], T.yb[:, col:col + W]
+        done = T.sem.cv if k % 2 == 0 else T.sem.ca
+        if k >= 8:
+            g.tensor.wait_ge(done, (k - 8) // 2 + 1)
+        g.tensor.matmul_mx(ps, T.qc[:, :], T.qs[:, :], c, s, True, True).then_inc(T.sem.mm, 1)
+        if k % 2 == 0:
+            g.vector.wait_ge(T.sem.mm, k + 1)
+            g.vector.tensor_copy(yb, ps).then_inc(done, 1)
+        else:
+            g.scalar.wait_ge(T.sem.mm, k + 1)
+            g.scalar.activation(yb, ps, ActivationFunctionType.Copy).then_inc(done, 1)
+        g.sync.wait_ge(done, k // 2 + 1)
+        g.sync.dma_start(T.y[:, col:col + W], yb).then_inc(T.sem.out, 16)
+    g.sync.wait_ge(T.sem.out, 16 * len(order))

import numpy as np
from concourse.mybir import dt, AluOpType, ActivationFunctionType

NT = 2
W = 128
SIM = 112
F = float(np.float32(1.3))
HALF = W // 2
PIECES = ["c0", "p", "c1"]

SCRATCH = {
    "kin": ("sbuf", [128, NT * W], "float8_e4m3fn_x4"),
    "kins": ("sbuf", [128, NT * W], "uint8"),
    "w": ("sbuf", [128, HALF], "bfloat16"),
    "e": ("sbuf", [128, 4 * W + 4], "bfloat16"),
    "sc": ("sbuf", [128, 4 * W], "float8_e4m3fn_x4"),
    "ss": ("sbuf", [128, 4 * W], "uint8"),
    "h": ("sbuf", [128, 4 * NT * W], "bfloat16"),
    "kq": ("sbuf", [128, NT * W], "float8_e4m3fn_x4"),
    "kqs": ("sbuf", [128, NT * W], "uint8"),
    "rc": ("sbuf", [128, NT * W], "float8_e4m3fn_x4"),
    "rs": ("sbuf", [128, NT * W], "uint8"),
    "qb": ("sbuf", [128, 4 * W], "bfloat16"),
    "qc": ("sbuf", [128, W], "float8_e4m3fn_x4"),
    "qs": ("sbuf", [128, W], "uint8"),
    "lc": ("sbuf", [128, 6 * NT * W], "float8_e4m3fn_x4"),
    "ls": ("sbuf", [128, 6 * NT * W], "uint8"),
    "yb": ("sbuf", [128, 6 * NT * W], "float32"),
    "ps": ("psum", [128, 8 * 512], "float32"),
}
SEMAPHORES = (["zero", "cnt", "diag", "sel", "kp", "mm", "hv", "ha", "quant", "sent", "qin", "qq", "cv", "ca", "out"]
              + ["kc%d" % i for i in range(NT)] + ["relay_" + x for x in PIECES]
              + ["arr%d_%s" % (r, x) for r in range(6) for x in PIECES])


def engines(topo, src, dst, piece):
    m = topo.mask(src, dst)
    for x in range(SIM):
        if topo.chip(x) != topo.chip(src) and topo.may_write(src, x):
            m &= topo.mask(src, x)
            break
    bits = [b for b in range(16) if m >> b & 1]
    return sum(1 << b for b in bits[(1 if piece == "c1" else 0)::2])


def count(mask):
    return bin(mask).count("1")


def roads_of(topo, cores, o, prods):
    far, near, road = 0, 0, {}
    gates = [x for x in range(SIM) if topo.mates(topo.chip(x), topo.chip(o)) and topo.may_write(x, o)]
    for r in prods:
        p = cores[r]
        other = [x for x in range(SIM) if topo.chip(x) == topo.chip(p) and topo.die(x) != topo.die(p)
                 and topo.may_write(x, o)]
        for x in PIECES:
            road[r, x] = None
        if topo.may_write(p, o):
            if near == 0:
                road[r, "c0"] = other[0]
            near += 1
        else:
            same = far % 2 == 1
            gate = [x for x in gates if (topo.die(x) == topo.die(o)) == same][0]
            for x in PIECES:
                road[r, x] = other[0] if x == "c0" and not same else gate
            far += 1
    return road


def rank_program(g, core, T, topo):
    cores, own = T.cores, T.tables["OWN"]
    rank = T.rank_of(core)

    def send(out, in_, rsem, dst, piece):
        rid, pid, _ = topo.addr(dst)
        m = engines(topo, core, dst, piece)
        g.remote_dma(out, in_, T.sem[rsem], T.sem.sent, pid, rid, m)
        return count(m)

    def view(codes, planes, at, piece):
        if piece == "p":
            return planes[:, at:at + NT * W]
        a = at + int(piece[1:]) * W
        return codes[:, a:a + W].bitcast(dt.uint8)

    def prods_of(o):
        return [r for r in range(len(cores)) if r != o and own[r] == o]

    if rank is None:
        n = 0
        for o in range(len(cores)):
            if own[o] != o:
                continue
            road = roads_of(topo, cores, cores[o], prods_of(o))
            for x in PIECES:
                for r in prods_of(o):
                    if road[r, x] == core:
                        g.wait_ge(T.sem["relay_" + x], count(engines(topo, cores[r], core, x)))
                        n += send(view(T.lc, T.ls, r * NT * W, x), view(T.rc, T.rs, 0, x), "arr%d_%s" % (r, x),
                                  cores[o], x)
        if n:
            g.wait_ge(T.sem.sent, n)
        return

    if own[rank] == rank:
        consumer(g, T, topo, rank, core, prods_of(rank))
        return
    make(g, T)
    o = cores[own[rank]]
    road, n = roads_of(topo, cores, o, prods_of(own[rank])), 0
    for x in PIECES:
        g.wait_ge(T.sem.quant, 1 if x == "c0" else NT)
        via, src = road[rank, x], view(T.kq, T.kqs, 0, x)
        if via is None:
            n += send(view(T.lc, T.ls, rank * NT * W, x), src, "arr%d_%s" % (rank, x), o, x)
        else:
            n += send(view(T.rc, T.rs, 0, x), src, "relay_" + x, via, x)
    g.wait_ge(T.sem.sent, n)


def load_k(g, T):
    kin, kc = T.kin, T.kc
    for i in range(NT):
        g.sync.dma_start(kin[:, i * W:(i + 1) * W].bitcast(dt.uint8),
                         kc[:, 4 * i * W:4 * (i + 1) * W]).then_inc(T.sem["kc%d" % i], 16)
    g.scalar.dma_start(T.kins[:, :], T.ks[:, :]).then_inc(T.sem.kp, 16)


def make(g, T):
    load_k(g, T)
    g.iota(T.w[:, :], [[-1, HALF]], 0, 1, allow_small_or_imprecise_dtypes=True).then_inc(T.sem.cnt, 1)
    g.vector.memset(T.e[:, :], 0.0).then_inc(T.sem.zero, 1)
    g.vector.wait_ge(T.sem.zero, 1)
    g.vector.wait_ge(T.sem.cnt, 1)
    for a in range(2):
        at = 3 + 4 * HALF * a
        g.vector.tensor_scalar(T.e[:, at:at + 4 * HALF:4], T.w[:, :], float(HALF * a), None,
                               AluOpType.is_equal).then_inc(T.sem.diag, 1)
    g.vector.wait_ge(T.sem.diag, 2)
    for b in range(4):
        g.vector.quantize_mx(T.sc[:, b * W:(b + 1) * W], T.ss[:, b * W:(b + 1) * W],
                             T.e[:, 3 - b:3 - b + 4 * W]).then_inc(T.sem.sel, 1)
    g.tensor.wait_ge(T.sem.kp, 16)
    for i in range(NT):
        g.tensor.wait_ge(T.sem["kc%d" % i], 16)
        for b in range(4):
            if i == 0:
                g.tensor.wait_ge(T.sem.sel, b + 1)
            at = (4 * i + b) * 512
            g.tensor.matmul_mx(T.ps[:, at:at + W], T.sc[:, b * W:(b + 1) * W], T.ss[:, b * W:(b + 1) * W],
                               T.kin[:, i * W:(i + 1) * W], T.kins[:, i * W:(i + 1) * W], True, True).then_inc(T.sem.mm, 1)
    for i in range(NT):
        for b in range(4):
            at, to = (4 * i + b) * 512, 4 * i * W
            out, in_ = T.h[:, to + b:to + 4 * W:4], T.ps[:, at:at + W]
            if b % 2 == 0:
                g.vector.wait_ge(T.sem.mm, 4 * i + b + 1)
                g.vector.tensor_scalar(out, in_, F, None, AluOpType.mult).then_inc(T.sem.hv, 1)
            else:
                g.scalar.wait_ge(T.sem.mm, 4 * i + b + 1)
                g.scalar.activation(out, in_, ActivationFunctionType.Copy, scale=F).then_inc(T.sem.ha, 1)
        g.vector.wait_ge(T.sem.hv, 2 * (i + 1))
        g.vector.wait_ge(T.sem.ha, 2 * (i + 1))
        g.vector.quantize_mx(T.kq[:, i * W:(i + 1) * W], T.kqs[:, i * W:(i + 1) * W],
                             T.h[:, 4 * i * W:4 * (i + 1) * W]).then_inc(T.sem.quant, 1)


def consumer(g, T, topo, rank, core, prods):
    g.scalar.dma_start(T.qb[:, :], T.q[:, :]).then_inc(T.sem.qin, 16)
    load_k(g, T)
    g.vector.wait_ge(T.sem.qin, 16)
    g.vector.quantize_mx(T.qc[:, :], T.qs[:, :], T.qb[:, :]).then_inc(T.sem.qq, 1)
    road = roads_of(topo, T.cores, core, prods)
    tiles = [(r, i) for i in range(NT) for r in prods]
    order = ([(rank, i) for i in range(NT)] + [t for t in tiles if road[t[0], "c%d" % t[1]] is None]
             + [t for t in tiles if road[t[0], "c%d" % t[1]] is not None])
    place = [rank] + prods
    g.tensor.wait_ge(T.sem.qq, 1)
    g.tensor.wait_ge(T.sem.kp, 16)
    for k, (r, i) in enumerate(order):
        if r == rank:
            g.tensor.wait_ge(T.sem["kc%d" % i], 16)
            c, s = T.kin[:, i * W:(i + 1) * W], T.kins[:, i * W:(i + 1) * W]
        else:
            for x in ("p", "c%d" % i):
                src = T.cores[r] if road[r, x] is None else road[r, x]
                g.tensor.wait_ge(T.sem["arr%d_%s" % (r, x)], count(engines(topo, src, core, x)))
            at = (r * NT + i) * W
            c, s = T.lc[:, at:at + W], T.ls[:, at:at + W]
        bank, col = (k % 8) * 512, (place.index(r) * NT + i) * W
        ps, yb = T.ps[:, bank:bank + W], T.yb[:, col:col + W]
        done = T.sem.cv if k % 2 == 0 else T.sem.ca
        if k >= 8:
            g.tensor.wait_ge(done, (k - 8) // 2 + 1)
        g.tensor.matmul_mx(ps, T.qc[:, :], T.qs[:, :], c, s, True, True).then_inc(T.sem.mm, 1)
        if k % 2 == 0:
            g.vector.wait_ge(T.sem.mm, k + 1)
            g.vector.tensor_copy(yb, ps).then_inc(done, 1)
        else:
            g.scalar.wait_ge(T.sem.mm, k + 1)
            g.scalar.activation(yb, ps, ActivationFunctionType.Copy).then_inc(done, 1)
        g.sync.wait_ge(done, k // 2 + 1)
        g.sync.dma_start(T.y[:, col:col + W], yb).then_inc(T.sem.out, 16)
    g.sync.wait_ge(T.sem.out, 16 * len(order))
